import numpy as np
import ml_dtypes

BF16 = ml_dtypes.bfloat16


def bf(x):
    return np.asarray(x, np.float32).astype(BF16)


def f32(x):
    return np.asarray(x, np.float32)


def f64(x):
    return np.asarray(x).astype(np.float64)


def striped(idx):
    return np.concatenate([l.reshape(-1, 16).T for l in idx])


def rows(idx, k):
    return np.tile(np.repeat(idx, 16, axis=0), (k // (16 * 8), 1))


def look(tab, idx):
    return np.take_along_axis(f64(tab), rows(idx, len(tab)), axis=1)


K, S, V, N, M = 512, 2048, 2048, 2048, 512


def silu(v):
    return v / (1.0 + np.exp(-v))


def setup_inputs():
    return {"tab": f32(np.random.standard_normal((K, S))), "y": f32(np.random.standard_normal((K, V))), "w": bf(np.random.standard_normal((K, M)) / np.sqrt(K)), "offs": striped(np.stack([np.random.permutation(S)[:N] for _ in range(8)]))}


def reference(tab, y, w, offs):
    idx = np.stack([g.T.reshape(-1) for g in np.split(offs, 8)])
    t = look(tab, idx)
    x = silu(t) * f64(y)
    y = f64(w).T @ x
    return y

@@ -1,0 +1,64 @@
+import concourse.mybir as mybir
+
+F32, BF16, U16 = mybir.dt.float32, mybir.dt.bfloat16, mybir.dt.uint16
+SILU = mybir.ActivationFunctionType.Silu
+MULT = mybir.AluOpType.mult
+
+P = 128
+K, S, N, M = 512, 2048, 2048, 512
+R_BLOCKS = K // P
+M_BLOCKS = M // P
+PIECE = 512
+J_PIECES = N // PIECE
+OFFS_COLS = PIECE // 16
+
+FLOPS = 2 * K * M * N
+BYTES = 4 * K * S + 4 * K * N + 2 * K * M + 2 * P * (N // 16) + 4 * M * N
+
+
+def tile_lookup_gate_silu_none_kernel(tc, tab, y, w, offs, out):
+    nc = tc.nc
+    with (
+        tc.tile_pool(name="held", bufs=1) as held,
+        tc.tile_pool(name="work", bufs=4) as work,
+        tc.psum_pool(name="psum", bufs=8) as psum,
+    ):
+        lists = held.tile([P, N // 16], U16, name="lists")
+        nc.sync.dma_start(lists[:], offs)
+
+        windows = []
+        for r in range(R_BLOCKS):
+            window = held.tile([P, S], F32, name=f"window{r}")
+            nc.sync.dma_start(window[:], tab[r * P : (r + 1) * P, :])
+            windows.append(window)
+
+        weights = held.tile([P, R_BLOCKS, M], BF16, name="weights")
+        nc.sync.dma_start(weights[:], w.rearrange("(r p) m -> p r m", p=P))
+
+        streams = []
+        for j in range(J_PIECES):
+            stream = held.tile([P, R_BLOCKS, PIECE], F32, name=f"stream{j}")
+            columns = y[:, j * PIECE : (j + 1) * PIECE]
+            nc.sync.dma_start(stream[:], columns.rearrange("(r p) c -> p r c", p=P))
+            streams.append(stream)
+
+        for j in range(J_PIECES):
+            picked = lists[:, j * OFFS_COLS : (j + 1) * OFFS_COLS]
+            sums = [psum.tile([P, PIECE], F32, name=f"sum{m}", tag="sum") for m in range(M_BLOCKS)]
+            for r in range(R_BLOCKS):
+                gate = work.tile([P, PIECE], F32, name="gate")
+                nc.scalar.activation(gate[:], windows[r][:].indirect(picked), SILU)
+                x = work.tile([P, PIECE], BF16, name="x")
+                nc.vector.tensor_tensor(x[:], gate[:], streams[j][:, r, :], MULT)
+                for m in range(M_BLOCKS):
+                    nc.tensor.matmul(
+                        sums[m][:],
+                        weights[:, r, m * P : (m + 1) * P],
+                        x[:],
+                        start=r == 0,
+                        stop=r == R_BLOCKS - 1,
+                    )
+            for m in range(M_BLOCKS):
+                result = work.tile([P, PIECE], F32, name="result")
+                nc.vector.tensor_copy(result[:], sums[m][:])
+                nc.sync.dma_start(out[m * P : (m + 1) * P, j * PIECE : (j + 1) * PIECE], result[:])

@@ -10,6 +10,7 @@ R_BLOCKS = K // P
 M_BLOCKS = M // P
 PIECE = 512
 J_PIECES = N // PIECE
+HALF = N // 2
 OFFS_COLS = PIECE // 16
 
 FLOPS = 2 * K * M * N
@@ -20,45 +21,88 @@ def tile_lookup_gate_silu_none_kernel(tc, tab, y, w, offs, out):
     nc = tc.nc
     with (
         tc.tile_pool(name="held", bufs=1) as held,
-        tc.tile_pool(name="work", bufs=4) as work,
+        tc.tile_pool(name="work", bufs=R_BLOCKS * J_PIECES) as work,
         tc.psum_pool(name="psum", bufs=8) as psum,
     ):
         lists = held.tile([P, N // 16], U16, name="lists")
         nc.sync.dma_start(lists[:], offs)
 
-        windows = []
-        for r in range(R_BLOCKS):
+        zero = held.tile([P, 1], F32, name="zero")
+        nc.vector.memset(zero[:], 0.0)
+        silu_of_zero = held.tile([P, 1], F32, name="silu_of_zero")
+        nc.scalar.activation(silu_of_zero[:], zero[:], SILU)
+
+        windows, streams, gates, xs, sums = [], {}, {}, {}, {}
+
+        def load_window(r):
             window = held.tile([P, S], F32, name=f"window{r}")
             nc.sync.dma_start(window[:], tab[r * P : (r + 1) * P, :])
             windows.append(window)
 
-        weights = held.tile([P, R_BLOCKS, M], BF16, name="weights")
-        nc.sync.dma_start(weights[:], w.rearrange("(r p) m -> p r m", p=P))
+        def load_stream(half, r):
+            stream = held.tile([P, HALF], F32, name=f"stream{half}_{r}")
+            nc.sync.dma_start(stream[:], y[r * P : (r + 1) * P, half * HALF : (half + 1) * HALF])
+            streams[half, r] = stream
 
-        streams = []
-        for j in range(J_PIECES):
-            stream = held.tile([P, R_BLOCKS, PIECE], F32, name=f"stream{j}")
-            columns = y[:, j * PIECE : (j + 1) * PIECE]
-            nc.sync.dma_start(stream[:], columns.rearrange("(r p) c -> p r c", p=P))
-            streams.append(stream)
-
-        for j in range(J_PIECES):
+        def look_up(r, j):
+            gate = work.tile([P, PIECE], F32, name="gate")
             picked = lists[:, j * OFFS_COLS : (j + 1) * OFFS_COLS]
-            sums = [psum.tile([P, PIECE], F32, name=f"sum{m}", tag="sum") for m in range(M_BLOCKS)]
-            for r in range(R_BLOCKS):
-                gate = work.tile([P, PIECE], F32, name="gate")
-                nc.scalar.activation(gate[:], windows[r][:].indirect(picked), SILU)
-                x = work.tile([P, PIECE], BF16, name="x")
-                nc.vector.tensor_tensor(x[:], gate[:], streams[j][:, r, :], MULT)
-                for m in range(M_BLOCKS):
-                    nc.tensor.matmul(
-                        sums[m][:],
-                        weights[:, r, m * P : (m + 1) * P],
-                        x[:],
-                        start=r == 0,
-                        stop=r == R_BLOCKS - 1,
-                    )
+            nc.scalar.activation(gate[:], windows[r][:].indirect(picked), SILU)
+            gates[r, j] = gate
+
+        def multiply(r, j):
+            half, start = divmod(j * PIECE, HALF)
+            x = work.tile([P, PIECE], BF16, name="x")
+            nc.vector.tensor_tensor(x[:], gates[r, j][:], streams[half, r][:, start : start + PIECE], MULT)
+            xs[r, j] = x
+
+        def add_up(r, j):
+            if r == 0:
+                sums[j] = [psum.tile([P, PIECE], F32, name=f"sum{m}", tag="sum") for m in range(M_BLOCKS)]
+            for m in range(M_BLOCKS):
+                nc.tensor.matmul(
+                    sums[j][m][:],
+                    weights[:, r, m * P : (m + 1) * P],
+                    xs[r, j][:],
+                    start=r == 0,
+                    stop=r == R_BLOCKS - 1,
+                )
+
+        def write_out(j):
             for m in range(M_BLOCKS):
                 result = work.tile([P, PIECE], F32, name="result")
-                nc.vector.tensor_copy(result[:], sums[m][:])
+                if j < 2 or m % 2 == 0:
+                    nc.vector.tensor_copy(result[:], sums[j][m][:])
+                else:
+                    nc.scalar.copy(result[:], sums[j][m][:])
                 nc.sync.dma_start(out[m * P : (m + 1) * P, j * PIECE : (j + 1) * PIECE], result[:])
+
+        load_window(0)
+        load_stream(0, 0)
+        weights = held.tile([P, R_BLOCKS, M], BF16, name="weights")
+        nc.sync.dma_start(weights[:], w.rearrange("(r p) m -> p r m", p=P))
+        for r in range(1, R_BLOCKS):
+            load_window(r)
+            load_stream(0, r)
+        for r in range(R_BLOCKS):
+            load_stream(1, r)
+
+        for r in range(R_BLOCKS):
+            for j in range(3):
+                look_up(r, j)
+            for j in range(2):
+                multiply(r, j)
+                add_up(r, j)
+        multiply(0, 2)
+        write_out(0)
+        for r in range(1, R_BLOCKS):
+            multiply(r, 2)
+        write_out(1)
+        for r in range(R_BLOCKS):
+            add_up(r, 2)
+        for r in range(R_BLOCKS):
+            look_up(r, 3)
+            multiply(r, 3)
+            add_up(r, 3)
+        write_out(2)
+        write_out(3)

@@ -21,6 +21,7 @@ def tile_lookup_gate_silu_none_kernel(tc, tab, y, w, offs, out):
     nc = tc.nc
     with (
         tc.tile_pool(name="held", bufs=1) as held,
+        tc.tile_pool(name="gate", bufs=6) as gate_pool,
         tc.tile_pool(name="work", bufs=R_BLOCKS * J_PIECES) as work,
         tc.psum_pool(name="psum", bufs=8) as psum,
     ):
@@ -39,70 +40,76 @@ def tile_lookup_gate_silu_none_kernel(tc, tab, y, w, offs, out):
             nc.sync.dma_start(window[:], tab[r * P : (r + 1) * P, :])
             windows.append(window)
 
-        def load_stream(half, r):
-            stream = held.tile([P, HALF], F32, name=f"stream{half}_{r}")
-            nc.sync.dma_start(stream[:], y[r * P : (r + 1) * P, half * HALF : (half + 1) * HALF])
-            streams[half, r] = stream
+        def load_first_streams(r):
+            stream = held.tile([P, HALF], F32, name=f"stream_r{r}")
+            nc.sync.dma_start(stream[:], y[r * P : (r + 1) * P, :HALF])
+            for j in range(2):
+                streams[r, j] = stream[:, j * PIECE : (j + 1) * PIECE]
+
+        def load_last_streams(j):
+            stream = held.tile([P, R_BLOCKS, PIECE], F32, name=f"stream_j{j}")
+            columns = y[:, j * PIECE : (j + 1) * PIECE]
+            nc.sync.dma_start(stream[:], columns.rearrange("(r p) c -> p r c", p=P))
+            for r in range(R_BLOCKS):
+                streams[r, j] = stream[:, r, :]
 
         def look_up(r, j):
-            gate = work.tile([P, PIECE], F32, name="gate")
+            gate = gate_pool.tile([P, PIECE], F32, name="gate")
             picked = lists[:, j * OFFS_COLS : (j + 1) * OFFS_COLS]
             nc.scalar.activation(gate[:], windows[r][:].indirect(picked), SILU)
             gates[r, j] = gate
 
         def multiply(r, j):
-            half, start = divmod(j * PIECE, HALF)
             x = work.tile([P, PIECE], BF16, name="x")
-            nc.vector.tensor_tensor(x[:], gates[r, j][:], streams[half, r][:, start : start + PIECE], MULT)
+            engine = nc.vector if j != 2 else nc.gpsimd
+            engine.tensor_tensor(x[:], gates[r, j][:], streams[r, j], MULT)
             xs[r, j] = x
 
-        def add_up(r, j):
+        def add_up(r, j, m):
             if r == 0:
-                sums[j] = [psum.tile([P, PIECE], F32, name=f"sum{m}", tag="sum") for m in range(M_BLOCKS)]
-            for m in range(M_BLOCKS):
-                nc.tensor.matmul(
-                    sums[j][m][:],
-                    weights[:, r, m * P : (m + 1) * P],
-                    xs[r, j][:],
-                    start=r == 0,
-                    stop=r == R_BLOCKS - 1,
-                )
+                sums[j, m] = psum.tile([P, PIECE], F32, name=f"sum{j}_{m}", tag="sum")
+            nc.tensor.matmul(
+                sums[j, m][:],
+                weights[:, r, m * P : (m + 1) * P],
+                xs[r, j][:],
+                start=r == 0,
+                stop=r == R_BLOCKS - 1,
+            )
 
-        def write_out(j):
-            for m in range(M_BLOCKS):
-                result = work.tile([P, PIECE], F32, name="result")
-                if j < 2 or m % 2 == 0:
-                    nc.vector.tensor_copy(result[:], sums[j][m][:])
-                else:
-                    nc.scalar.copy(result[:], sums[j][m][:])
-                nc.sync.dma_start(out[m * P : (m + 1) * P, j * PIECE : (j + 1) * PIECE], result[:])
+        def write_out(j, m):
+            result = work.tile([P, PIECE], F32, name="result")
+            if j < 3 or m % 2 == 0:
+                nc.vector.tensor_copy(result[:], sums[j, m][:])
+            else:
+                nc.scalar.copy(result[:], sums[j, m][:])
+            nc.sync.dma_start(out[m * P : (m + 1) * P, j * PIECE : (j + 1) * PIECE], result[:])
 
         load_window(0)
-        load_stream(0, 0)
+        load_first_streams(0)
         weights = held.tile([P, R_BLOCKS, M], BF16, name="weights")
         nc.sync.dma_start(weights[:], w.rearrange("(r p) m -> p r m", p=P))
         for r in range(1, R_BLOCKS):
             load_window(r)
-            load_stream(0, r)
-        for r in range(R_BLOCKS):
-            load_stream(1, r)
+            load_first_streams(r)
+        for j in range(2, J_PIECES):
+            load_last_streams(j)
 
         for r in range(R_BLOCKS):
             for j in range(3):
                 look_up(r, j)
             for j in range(2):
                 multiply(r, j)
-                add_up(r, j)
-        multiply(0, 2)
-        write_out(0)
-        for r in range(1, R_BLOCKS):
-            multiply(r, 2)
-        write_out(1)
-        for r in range(R_BLOCKS):
-            add_up(r, 2)
-        for r in range(R_BLOCKS):
-            look_up(r, 3)
-            multiply(r, 3)
-            add_up(r, 3)
-        write_out(2)
-        write_out(3)
+                for m in range(M_BLOCKS):
+                    add_up(r, j, m)
+        for j in range(2):
+            for m in range(M_BLOCKS):
+                write_out(j, m)
+        for j in range(2, J_PIECES):
+            for r in range(R_BLOCKS):
+                if j == 3:
+                    look_up(r, j)
+                multiply(r, j)
+                for m in range(M_BLOCKS):
+                    add_up(r, j, m)
+            for m in range(M_BLOCKS):
+                write_out(j, m)

import concourse.mybir as mybir

F32, BF16, U16 = mybir.dt.float32, mybir.dt.bfloat16, mybir.dt.uint16
SILU = mybir.ActivationFunctionType.Silu
MULT = mybir.AluOpType.mult

P = 128
K, S, N, M = 512, 2048, 2048, 512
R_BLOCKS = K // P
M_BLOCKS = M // P
PIECE = 512
J_PIECES = N // PIECE
HALF = N // 2
OFFS_COLS = PIECE // 16

FLOPS = 2 * K * M * N
BYTES = 4 * K * S + 4 * K * N + 2 * K * M + 2 * P * (N // 16) + 4 * M * N


def tile_lookup_gate_silu_none_kernel(tc, tab, y, w, offs, out):
    nc = tc.nc
    with (
        tc.tile_pool(name="held", bufs=1) as held,
        tc.tile_pool(name="gate", bufs=6) as gate_pool,
        tc.tile_pool(name="work", bufs=R_BLOCKS * J_PIECES) as work,
        tc.psum_pool(name="psum", bufs=8) as psum,
    ):
        lists = held.tile([P, N // 16], U16, name="lists")
        nc.sync.dma_start(lists[:], offs)

        zero = held.tile([P, 1], F32, name="zero")
        nc.vector.memset(zero[:], 0.0)
        silu_of_zero = held.tile([P, 1], F32, name="silu_of_zero")
        nc.scalar.activation(silu_of_zero[:], zero[:], SILU)

        windows, streams, gates, xs, sums = [], {}, {}, {}, {}

        def load_window(r):
            window = held.tile([P, S], F32, name=f"window{r}")
            nc.sync.dma_start(window[:], tab[r * P : (r + 1) * P, :])
            windows.append(window)

        def load_first_streams(r):
            stream = held.tile([P, HALF], F32, name=f"stream_r{r}")
            nc.sync.dma_start(stream[:], y[r * P : (r + 1) * P, :HALF])
            for j in range(2):
                streams[r, j] = stream[:, j * PIECE : (j + 1) * PIECE]

        def load_last_streams(j):
            stream = held.tile([P, R_BLOCKS, PIECE], F32, name=f"stream_j{j}")
            columns = y[:, j * PIECE : (j + 1) * PIECE]
            nc.sync.dma_start(stream[:], columns.rearrange("(r p) c -> p r c", p=P))
            for r in range(R_BLOCKS):
                streams[r, j] = stream[:, r, :]

        def look_up(r, j):
            gate = gate_pool.tile([P, PIECE], F32, name="gate")
            picked = lists[:, j * OFFS_COLS : (j + 1) * OFFS_COLS]
            nc.scalar.activation(gate[:], windows[r][:].indirect(picked), SILU)
            gates[r, j] = gate

        def multiply(r, j):
            x = work.tile([P, PIECE], BF16, name="x")
            engine = nc.vector if j != 2 else nc.gpsimd
            engine.tensor_tensor(x[:], gates[r, j][:], streams[r, j], MULT)
            xs[r, j] = x

        def add_up(r, j, m):
            if r == 0:
                sums[j, m] = psum.tile([P, PIECE], F32, name=f"sum{j}_{m}", tag="sum")
            nc.tensor.matmul(
                sums[j, m][:],
                weights[:, r, m * P : (m + 1) * P],
                xs[r, j][:],
                start=r == 0,
                stop=r == R_BLOCKS - 1,
            )

        def write_out(j, m):
            result = work.tile([P, PIECE], F32, name="result")
            if j < 3 or m % 2 == 0:
                nc.vector.tensor_copy(result[:], sums[j, m][:])
            else:
                nc.scalar.copy(result[:], sums[j, m][:])
            nc.sync.dma_start(out[m * P : (m + 1) * P, j * PIECE : (j + 1) * PIECE], result[:])

        load_window(0)
        load_first_streams(0)
        weights = held.tile([P, R_BLOCKS, M], BF16, name="weights")
        nc.sync.dma_start(weights[:], w.rearrange("(r p) m -> p r m", p=P))
        for r in range(1, R_BLOCKS):
            load_window(r)
            load_first_streams(r)
        for j in range(2, J_PIECES):
            load_last_streams(j)

        for r in range(R_BLOCKS):
            for j in range(3):
                look_up(r, j)
            for j in range(2):
                multiply(r, j)
                for m in range(M_BLOCKS):
                    add_up(r, j, m)
        for j in range(2):
            for m in range(M_BLOCKS):
                write_out(j, m)
        for j in range(2, J_PIECES):
            for r in range(R_BLOCKS):
                if j == 3:
                    look_up(r, j)
                multiply(r, j)
                for m in range(M_BLOCKS):
                    add_up(r, j, m)
            for m in range(M_BLOCKS):
                write_out(j, m)
